import numpy as np, ml_dtypes
CORES = [2,3,42,43,82,83,122,123]
N = 8
BF = ml_dtypes.bfloat16
def gentries(a):
    return np.ascontiguousarray(a.reshape(8, 16, -1).transpose(0, 2, 1)).reshape(8, -1)
def gtable(e):
    e = np.asarray(e); return np.ascontiguousarray(e.reshape(8, -1, 16).transpose(0, 2, 1)).reshape(128, -1).astype(np.int32)
V, R, L, S = 4096, 256, 8, 1
def trees(rng, deep):
    T = N * 8; ar = np.arange(T); P = V // 2 - 1; i = np.arange(P)[:, None]
    pair = 2 * (np.argsort(rng.random((T, P)), axis=1) + 1); side = rng.integers(0, 2, (P, T))
    pick = np.where(rng.random((P, T)) < deep, i, np.minimum((rng.random((P, T)) * (i + 1)).astype(np.int64), i))
    kid = np.full((T, V), -1, np.int64); up = np.zeros((T, V), np.int64); leaf = np.zeros((T, P + 1), np.int64); cnt = np.ones((T, V), np.int64)
    for t in range(P):
        j = pick[t]; n = leaf[ar, j]; k = pair[:, t]; b = side[t]
        kid[ar, n] = k; up[ar, k] = n; up[ar, k + 1] = n
        leaf[ar, j] = k + b; leaf[ar, t + 1] = k + 1 - b
    for t in range(P - 1, -1, -1):
        k = pair[:, t]; cnt[ar, up[ar, k]] = cnt[ar, k] + cnt[ar, k + 1]
    return kid, up, cnt
def quads(rng, kid, cnt, top, drop):
    T = N * 8; Q = 4 * R; ar = np.arange(T)[:, None]; ar3 = ar[:, :, None]
    ok = cnt >= 4; order = np.argsort(~ok, axis=1, kind="stable"); num = np.sum(ok, axis=1)[:, None]
    x = order[ar, np.minimum((rng.random((T, Q)) * num).astype(np.int64), num - 1)]
    c = np.full((T, Q, 4), -1, np.int64); c[:, :, 0] = np.where(rng.random((T, Q)) < top, 0, x)
    for w in (1, 2, 3):
        k = kid[ar3, np.maximum(c, 0)]
        t = np.argmax(np.where((c >= 0) & (k >= 0), rng.random(c.shape), -1.0), axis=2)[..., None]
        k = np.take_along_axis(k, t, 2); np.put_along_axis(c, t, k, 2); c[:, :, w] = k[..., 0] + 1
    m = rng.random((T, Q, 1)) < drop
    for w in range(4):
        k = kid[ar3, c]; go = m & (k >= 0) & (rng.random(c.shape) < 0.3)
        c = np.where(go, k + rng.integers(0, 2, c.shape), c)
    return np.take_along_axis(c, np.argsort(rng.random(c.shape), axis=2), 2)
def parts(rng, deep=0.2, top=0.15, drop=0.5):
    kid, up, cnt = trees(rng, deep)
    return {"s": rng.integers(0, 256, (N, 8, 16, V)), "m": rng.integers(0, 256, (N, 8, 16, V)), "kid": kid, "up": up,
            "a": rng.integers(0, 256, (N, 8, 16, R)), "a0": rng.integers(0, 256, (N, 8, 16, R)), "lk": rng.integers(0, R, (N, 8, L, R)), "cut0": quads(rng, kid, cnt, top, drop)}
def pack(d):
    q = {}
    for k in ("s", "m", "kid", "up", "a", "a0", "lk", "cut0"):
        v = d[k]
        if k in ("kid", "up"): q[k] = np.ascontiguousarray(v.reshape(N, 8, V)).astype(np.int32)
        elif k in ("lk", "cut0"): q[k] = np.stack([gtable(x) for x in v.reshape(N, 8, -1)])
        else: q[k] = np.ascontiguousarray(v.reshape(N, 128, -1)).astype(np.float32).astype(BF)
    return q
def setup_inputs(rng):
    return pack(parts(rng))
def setup_inputs_ties(rng):
    d = parts(rng, 0.2, 0.3, 0.4)
    d["a"] = rng.integers(1, 3, (N, 8, 16, R)); d["a0"] = rng.integers(1, 3, (N, 8, 16, R))
    d["s"] = np.repeat(rng.integers(0, 3, (N, 8, 1, V)) * rng.choice(np.array([1, 7, 100]), (N, 8, 1, 1)), 16, axis=2)
    d["s"][:, 3] = 7; d["s"][:, 5] = np.where(rng.random((N, 16, V)) < 0.5, 1, 2)
    return pack(d)
def setup_inputs_deep(rng):
    T = N * 8; Q = 4 * R; deep = rng.choice(np.array([0.0, 0.9, 1.0]), (1, T)); deep[0, 0] = 1.0; deep[0, T - 1] = 0.0
    d = parts(rng, deep, 0.05, 0.3); n = np.arange(V)[None, :]
    leaf = np.argsort(np.where((d["kid"] < 0) & (n != 1), n, V + n), axis=1)[:, :V // 2]
    at = rng.integers(0, V // 2 - 3, (T, Q)); at[:, 0] = 0; at[:, 1] = V // 2 - 4
    m = rng.random((T, Q)) < 0.4; m[:, :2] = True
    four = leaf[np.arange(T)[:, None, None], at[:, :, None] + np.arange(4)]
    four = np.take_along_axis(four, np.argsort(rng.random(four.shape), axis=2), 2)
    d["cut0"] = np.where(m[:, :, None], four, d["cut0"])
    return pack(d)
def top_end(rng, d, g):
    ar = np.arange(N); c = d["cut0"].reshape(N, 8, R, 4, 4).copy(); k = d["kid"].reshape(N, 8, V)[:, g]; u = d["up"].reshape(N, 8, V)[:, g]
    q = c[:, g].reshape(N, 4 * R, 4); sib = np.any(q[..., None, :] == (q ^ 1)[..., :, None], axis=3)
    q = np.take_along_axis(q, np.argsort(~sib, axis=2, kind="stable"), 2)
    inner = k[ar[:, None, None], q] >= 0; good = (np.sum(sib, axis=2) == 2) & inner[..., 2] & inner[..., 3]
    p = q[ar, np.argmax(good, axis=1)]
    c[:, g] = q.reshape(N, R, 4, 4); c[:, g, ::2, 0] = p[:, None, :]; d["cut0"] = c
    j = rng.integers(0, 16, (N, V))
    j[ar, p[:, 0]] = 2; j[ar, p[:, 1]] = 2; j[ar, u[ar, p[:, 0]]] = 2; j[ar, p[:, 2]] = 1; j[ar, p[:, 3]] = 1
    d["s"][:, g] = 255 - (np.arange(16)[None, :, None] == j[:, None, :]).astype(np.int64)
    d["a"][:, g] = rng.integers(254, 256, (N, 16, R)); d["a"][:, g, 12:] = 255; d["a"][:, g, 1, ::2] = 254; d["a"][:, g, 2, ::2] = 255
    d["a0"][:, g] = rng.integers(0, 2, (N, 16, R))
def setup_inputs_ends(rng):
    d = parts(rng)
    for k in ("s", "m", "a", "a0"):
        e = rng.random(d[k].shape); d[k] = np.where(e < 0.4, 255, np.where(e < 0.7, 0, d[k]))
    for k in ("s", "m", "a"): d[k][:, 0] = 255
    d["a"][:, 1, :, ::2] = 0; d["s"][:, 2] = 0
    d["lk"][:, ::2] = rng.choice(np.array([0, R - 1]), (N, 4, L, R))
    top_end(rng, d, 7)
    return pack(d)
def setup_inputs_alike(rng):
    d = parts(rng, 0.0, 1.0, 0.2)
    d["lk"][:, 1::2] = rng.integers(0, R, (N, 4, 1, 1))
    c = d["cut0"].reshape(N, 8, R, 16).copy(); c[:, ::2] = c[:, ::2, :1].copy(); d["cut0"] = c
    d["a"][:, :4] = np.repeat(d["a"][:, :4, :, :R // 16], 16, axis=3); d["a0"][:, 2:6, :, :R // 2] = d["a"][:, 2:6, :, :R // 2]
    return pack(d)
def setup_inputs_spread(rng):
    d = parts(rng)
    for k in ("s", "m", "a", "a0"):
        n = d[k].shape[3]; d[k] = np.floor(np.exp2(8 * rng.random((N, 8, 1, n))) * rng.random((N, 8, 16, n))).astype(np.int64)
    return pack(d)
def check_inputs(d):
    bad = []
    for k in ("s", "m", "a", "a0"):
        x = np.asarray(d[k]).astype(np.float32)
        if not np.all((x >= 0) & (x <= 255) & (x == np.floor(x))): bad.append("numbers of " + k)
    if np.min(d["lk"]) < 0 or np.max(d["lk"]) > R - 1: bad.append("range of lk")
    if np.min(d["cut0"]) < 2 or np.max(d["cut0"]) > V - 1: bad.append("range of cut0")
    T = N * 8; kid = np.asarray(d["kid"]).astype(np.int64).reshape(T, V); up = np.asarray(d["up"]).astype(np.int64).reshape(T, V)
    if np.min(kid) < -1 or np.max(kid) > V - 1 or np.min(up) < 0 or np.max(up) > V - 1: return bad + ["range of the trees"]
    ar = np.arange(T)[:, None]; n = np.arange(V)[None, :]
    ok = np.all(up[:, :2] == 0) and np.all(kid[:, 1] == -1) and np.all((kid == -1) | ((kid >= 2) & (kid % 2 == 0)))
    ok = ok and np.all(kid[ar, up][:, 2:] == (n - n % 2)[:, 2:]) and np.all(up[:, 0::2] == up[:, 1::2])
    ok = ok and np.all((kid < 0) | (up[ar, np.maximum(kid, 0)] == n))
    jump = [up]; dep = np.where(n == 0, 0, 1) + np.zeros((T, 1), np.int64); K = V.bit_length()
    for k in range(K):
        dep = dep + dep[ar, jump[-1]]; jump.append(jump[-1][ar, jump[-1]])
    if not ok or np.any(jump[-1]): return bad + ["trees"]
    if "range of cut0" in bad: return bad
    c = np.stack([gentries(np.asarray(x)) for x in d["cut0"]]).astype(np.int64).reshape(T, 4 * R, 4); wrong = False
    for i in range(4):
        for j in range(i):
            x, y = c[:, :, i], c[:, :, j]; dx, dy = dep[ar, x], dep[ar, y]
            low = np.where(dx >= dy, x, y); high = np.where(dx >= dy, y, x); dif = np.abs(dx - dy)
            for k in range(K): low = np.where(((dif >> k) & 1) > 0, jump[k][ar, low], low)
            wrong = wrong or bool(np.any(low == high))
    if wrong: bad.append("quads of cut0")
    return bad
def reference(s, m, kid, up, a, a0, lk, cut0):
    def rows(x, n): return np.ascontiguousarray(x.astype(np.float32).astype(np.int64).reshape(N, 8, 16, n).transpose(0, 1, 3, 2))
    sv, mv, av, ka = rows(s, V), rows(m, V), rows(a, R), rows(a0, R)
    kd, pu = kid.astype(np.int64), up.astype(np.int64)
    lv = np.stack([gentries(x) for x in lk]).astype(np.int64).reshape(N, 8, L, R)
    cut = np.stack([gentries(x) for x in cut0]).astype(np.int64).reshape(N, 8, R, 4, 4)
    G3 = np.arange(8)[:, None, None]; G4 = G3[..., None]; E = np.zeros((N, 8, R, 16), np.int64)
    def at(x, i): return np.take_along_axis(x, i, 3)
    for h in range(N):
        newcut = []; newa = []
        for r in range(N):
            b = (r - h) % N; x = av[b]; w = lv[b]
            dist = np.sum(np.abs(x[:, None] - ka[r][G3, w]).reshape(8, L, R, 4, 4), axis=4)
            best = np.argmin(dist, axis=1)
            own = w[G3, best, np.arange(R)[None, :, None]]
            c = cut[r][G3, own, np.arange(4)[None, None, :]]
            xx = x[:, :, None, None, :]
            for step in range(S):
                k = kd[r][G4, c]; p = pu[r][G4, c]
                err = np.where(k >= 0, np.sum(sv[r][G4, c] * xx, axis=4), -1)
                cost = np.sum(sv[r][G4, p] * xx, axis=4)
                i = np.argmax(err, axis=3)[..., None]; free = np.arange(4) != i
                mate = (c[..., None, :] == (c ^ 1)[..., :, None]) & free[..., None, :] & free[..., :, None]
                pair = np.any(mate, axis=4); j = np.argmax(pair, axis=3)[..., None]
                j2 = np.argmax(np.take_along_axis(mate, j[..., None], 3)[..., 0, :], axis=3)[..., None]
                go = np.any(pair, axis=3)[..., None] & (at(cost, j) < at(err, i)); left = at(k, i)
                new = c.copy()
                np.put_along_axis(new, i, left, 3); np.put_along_axis(new, j, at(p, j), 3); np.put_along_axis(new, j2, left + 1, 3)
                c = np.where(go, new, c)
            E[b] += x * np.sum(mv[r][G4, c], axis=(2, 3))
            newcut.append(c); newa.append(x)
        cut = np.stack(newcut); ka = np.stack(newa)
    return {"ye": np.ascontiguousarray(E.transpose(0, 1, 3, 2)).reshape(N, 128, R).astype(np.float32), "yc": np.stack([gtable(x.reshape(8, -1)) for x in cut]).astype(np.float32)}

from concourse.bass import DstId, RemoteDMATransfer
from concourse.mybir import AluOpType, ActivationFunctionType

NR = 8
PBG, CM, TOL = -5.0, 4, 0.05
BIG = 25165824.0

F32, B16, I32, U16 = "float32", "bfloat16", "int32", "uint16"
SCRATCH = {}
for _n, _w, _d in (
        ("idf", 128, F32), ("idb", 128, B16), ("nid", 128, F32), ("ones", 128, F32), ("ind", 32, F32), ("c2k", 16, B16),
        ("wk", 32, B16), ("wu", 32, B16), ("tio", 128, F32), ("tb", 128, F32), ("rs", 128, F32), ("kio", 128, F32),
        ("kc", 256, I32), ("uc", 256, I32), ("bu", 256, I32), ("uf", 128, F32), ("upl", 128, U16), ("lki", 128, I32),
        ("lku", 128, U16), ("kw", 128, F32), ("ci", 256, I32), ("f0", 256, F32), ("sraw", 4096, B16), ("st", 4096, B16),
        ("mt", 4096, B16), ("sp", 2048, B16), ("ku", 4096, B16), ("a0b", 256, B16),
        ("df", 2048, B16), ("da", 2048, B16), ("k3", 64, F32), ("q1", 64, I32), ("q2", 64, I32), ("q3", 64, I32),
        ("q4", 64, I32), ("oh", 64, U16), ("ys", 256, F32)):
    SCRATCH[_n] = ("sbuf", [128, _w], _d)
for _n, _s, _d in (("rm", [8, 128], B16), ("mkr", [8, 4096], B16), ("kt", [128, 4, 256], I32), ("kf", [128, 5, 256], B16),
                   ("ky", [128, 4, 128], F32), ("k1", [128, 4, 64], F32), ("k2", [128, 4, 32], F32)):
    SCRATCH[_n] = ("sbuf", _s, _d)
for _q in range(4):
    SCRATCH["bq%d" % _q] = ("sbuf", [128, 144], B16)
    SCRATCH["sel%d" % _q] = ("sbuf", [128, 32], F32)
for _b in range(NR):
    SCRATCH["al%d" % _b] = ("sbuf", [128, 256], B16)
    SCRATCH["ow%d" % _b] = ("sbuf", [128, 64], U16)
    SCRATCH["ms%d" % _b] = ("sbuf", [128, 256], F32)
for _b in range(1, NR):
    SCRATCH["el%d" % _b] = ("sbuf", [128, 256], F32)
for _p in range(2):
    for _n, _w, _d in (("ax", 2048, B16), ("ac", 512, B16), ("fw", 256, F32), ("gg", 512, F32), ("x", 256, F32),
                       ("qq", 256, B16), ("sl", 128, U16), ("pd", 2048, F32), ("lst", 96, U16), ("ko", 1024, B16),
                       ("pr", 512, F32), ("t3", 136, F32), ("ml", 128, U16), ("mg", 4096, B16), ("lk_", 132, F32),
                       ("ct", 132, F32), ("yy", 256, F32), ("w", 1536, F32)):
        SCRATCH["%s%d" % (_n, _p)] = ("sbuf", [128, _w], _d)
    SCRATCH["pa%d" % _p] = ("psum", [128, 32, 16], F32)
    SCRATCH["pb%d" % _p] = ("psum", [128, 512], F32)
    SCRATCH["pc%d" % _p] = ("psum", [128, 512], F32)
    SCRATCH["pe%d" % _p] = ("psum", [128, 32, 16], F32)

SEMAPHORES = ["cv", "cs", "ct", "cg", "loc"]
SEMAPHORES += ["aa%d" % b for b in range(NR)] + ["oo%d" % b for b in range(NR)] + ["ee%d" % h for h in range(1, NR)]
SEMAPHORES += ["d%d" % i for i in range(60)]

CTR = {"V": "cv", "A": "cs", "P": "ct", "G": "cg"}
WN = ["key", "mx", "Z", "um", "J", "S", "go", "zc", "ju", "mr", "d2", "d5"]
CY, GA, PY, HOP = 1.0e-3, 1.55e-3, 0.5e-3, 0.1


def rank_program(g, core, T, topo):
    rank = T.rank_of(core)
    if rank is None:
        return
    A, F = AluOpType, ActivationFunctionType
    ops = []
    lastw, readers, bank_last = {}, {}, {}
    BST = [0.0]

    def add(eng, fn, dur, r=(), w=(), banks=(), lat=0.0, sem=None):
        i = len(ops)
        deps = {}
        for k in r:
            if k in lastw:
                deps[lastw[k]] = True
        for k in w:
            if k in lastw:
                j = lastw[k]
                deps[j] = deps.get(j, False) or eng != "P" or ops[j]["eng"] != eng
            for j in readers.get(k, ()):
                deps[j] = True
        for b in banks:
            d = bank_last.setdefault(b, {})
            for e, j in d.items():
                deps[j] = deps.get(j, False) or e != eng
            d[eng] = i
        deps.pop(i, None)
        for k in r:
            readers.setdefault(k, []).append(i)
        for k in w:
            lastw[k] = i
            readers[k] = []
        ops.append({"eng": eng, "fn": fn, "dur": dur, "lat": lat, "deps": deps, "sem": sem, "pb": BST[0]})
        return i

    def V(fn, n, r=(), w=(), banks=()):
        return add("V", fn, max(64, n) * CY, r, w, banks)

    def VG(fn, n, r=(), w=(), banks=()):
        return add("V", fn, 0.06 + n * GA, r, w, banks)

    def S(fn, n, r=(), w=(), banks=()):
        return add("A", fn, 0.02 + max(64, n) * CY, r, w, banks)

    def SG(fn, n, r=(), w=(), banks=()):
        return add("A", fn, 0.08 + n * GA, r, w, banks)

    def P(fn, cyc, r=(), w=(), banks=()):
        return add("P", fn, cyc * PY, r, w, banks)

    def G(fn, n, r=(), w=()):
        return add("G", fn, 0.2 + 2 * n * CY, r, w)

    nd = [0]

    def D(out, in_, r=(), w=(), lat=2.5, eng="S"):
        s = "d%d" % nd[0]
        nd[0] += 1
        q = g.sync if eng == "S" else g.scalar
        return add(eng, lambda: q.dma_start(out, in_), 0.08, r, w, (), lat, s)

    def tt(out, a, b, op):
        return lambda: g.vector.tensor_tensor(out, a, b, op)

    def ts(out, a, s1, op):
        return lambda: g.vector.tensor_scalar(out, a, s1, None, op)

    def cp(out, a):
        return lambda: g.vector.tensor_copy(out, a)

    def ms(out, c):
        return lambda: g.vector.memset(out, c)

    def act(out, a, func=F.Copy, bias=0.0, scale=1.0):
        return lambda: g.scalar.activation(out, a, func, bias=bias, scale=scale)

    def mms(lst):
        def f():
            o = None
            for out, l, rr, st, sp in lst:
                o = g.tensor.matmul(out, l, rr, st, sp)
            return o
        return f

    def sel(out, in_, pat, op, fill, base, cm):
        return lambda: g.affine_select(out, in_, pat, op, fill, base, cm)

    others = [c for c in T.cores if c != core]
    common = [e for e in topo.engines(core, others[0])]
    for c in others:
        common = [e for e in common if e in topo.engines(core, c)]
    emask = 0
    for e in common:
        emask |= 1 << e
    ne = len(common)
    nloc = [0]

    def dst(c):
        rid, pid, _ = topo.addr(c)
        return DstId(rid=rid, pnc=pid)

    def bcast(buf, sem):
        def f():
            t = RemoteDMATransfer(dst_ids=[dst(c) for c in others], dma_engine_mask=emask, remote_sem=T.sem[sem],
                                  srcs=[T[buf][:]], dsts=[T[buf][:] for _ in others])
            g.remote_dma_fused([t], local_sem=T.sem.loc)
            nloc[0] += ne
        return f

    def send(c, src, to, sem):
        def f():
            rid, pid, _ = topo.addr(c)
            g.remote_dma(T[to][:], T[src][:], T.sem[sem], T.sem.loc, pid, rid, emask)
            nloc[0] += ne
        return f

    def arrive(key, sem, sent):
        add("X", None, 0.0, (sent,), (key,), (), 0.0, sem)

    me = "al%d" % rank
    nxt = (rank + 1) % NR

    D(T.kc[:], T.kid[:], w=("kc",))
    D(T.lki[:], T.lk[:], w=("lki",))
    D(T[me][:], T.a[:], w=(me,))
    D(T.a0b[:], T.a0[:], w=("a0b",))
    D(T.uc[:], T.up[:], w=("uc",))
    D(T.ci[:], T.cut0[:], w=("ci",))
    for i in range(8):
        D(T.bu[:, 32 * i:32 * i + 32], T.up[i:i + 1, :], w=("bu%d" % i,))
    D(T.sraw[:], T.s[:], w=("sraw",), lat=5.0)
    D(T.mt[:], T.m[:], w=("mt",), lat=6.0)
    add("G", bcast(me, "aa%d" % rank), 0.5, (me,), ("sa",), (), 4.0, "remote")
    for h in range(1, NR):
        b = (rank - h) % NR
        arrive("al%d" % b, "aa%d" % b, "sa")

    V(ms(T.ones[:], 1.0), 128, w=("ones",))
    V(ms(T.c2k[:], 2048.0), 16, w=("c2k",))
    for q in range(4):
        V(ms(T["bq%d" % q][:], 0.0), 72, w=("bq%d" % q,))
    for n, wd in (("wk", 16), ("wu", 16), ("rm", 64)):
        V(ms(T[n][:], 0.0), wd, w=(n,))
    for q in range(4):
        V(ms(T["sel%d" % q][:], 0.0), 32, w=("sel%d" % q,))
    V(ms(T.ku[:], 0.0), 2048, w=["ku%d" % f for f in range(4)])
    G(sel(T.idf[:], T.ones[:], [[-1, 128]], A.is_equal, 0.0, 0, 1), 128, ("ones",), ("idf",))
    for q in range(4):
        n = "bq%d" % q
        G(sel(T[n][:, 15::16], T.c2k[:, 0:9], [[16, 9]], A.is_ge, 0.0, 3 + 4 * q, -1), 9, ("c2k", n), (n,))
        G(sel(T[n][:, 15::16], T[n][:, 15::16], [[-16, 9]], A.is_ge, 0.0, -4 * q, 1), 9, (n,), (n,))
    G(lambda: g.iota(T.kio[:], [[256, 8], [0, 16]], 0, 0, allow_small_or_imprecise_dtypes=True), 128, (), ("kio",))
    G(sel(T.rm[:], T.rm[:], [[-1, 8], [0, 16]], A.not_equal, 1.0, 0, 1), 128, ("rm",), ("rm",))
    for q in range(4):
        n = "sel%d" % q
        G(sel(T[n][:], T[n][:], [[-16, 8], [-1, 4]], A.not_equal, 1.0, -4 * q, 1), 32, (n,), (n,))
    G(sel(T.ind[:], T.ones[:, 0:32], [[-16, 8], [0, 4]], A.is_ge, 0.0, 0, 1), 32, ("ones",), ("ind",))
    G(sel(T.ind[:], T.ind[:], [[16, 8], [0, 4]], A.is_ge, 0.0, 15, -1), 32, ("ind",), ("ind",))
    for f, n, v in ((0, "wk", 1.0), (1, "wk", 256.0), (2, "wu", 1.0), (3, "wu", 256.0)):
        G(sel(T[n][:], T[n][:], [[-16, 8], [0, 4]], A.not_equal, v, -f, 1), 32, (n,), (n,))
    G(lambda: g.iota(T.tio[:], [[0, 32], [1, 4]], 0, 0, allow_small_or_imprecise_dtypes=True), 128, (), ("tio",))
    V(ts(T.nid[:], T.idf[:], -1.0, A.mult), 128, ("idf",), ("nid",))
    V(cp(T.idb[:], T.idf[:]), 128, ("idf",), ("idb",))
    V(ts(T.tb[:], T.tio[:], -0.25, A.mult), 128, ("tio",), ("tb",))
    V(ts(T.rs[:], T.tio[:], 1.0, A.min), 128, ("tio",), ("rs",))

    def W(H, n):
        o = 128 * WN.index(n)
        return T["w%d" % H][:, o:o + 128]

    def fld(H, n, t):
        o = 128 * WN.index(n)
        return T["w%d" % H][:, o + t:o + 128:4]

    for H in range(2):
        h_ = str(H)
        V(ms(T["lk_" + h_][:], 0.0), 132, w=("LK0" + h_,))
        V(ms(T["ct" + h_][:], 0.0), 132, w=("CT" + h_,))
        V(ms(T["t3" + h_][:, 128:136], 0.0), 8, w=("T3p" + h_,))
        V(ms(fld(H, "J", 3), 0.0), 32, w=("J3" + h_,))
        V(ms(T["qq" + h_][:], 0.0), 128, w=["Q%d%s" % (t, h_) for t in range(4)])

    V(cp(T.lku[:], T.lki[:]), 128, ("lki",), ("lku",))
    V(tt(T.kw[:], T.lki[:], T.kio[:], A.add), 256, ("lki", "kio"), ("kw",))

    def choose(ka, pbank):
        for k in range(8):
            VG(tt(T.df[:, 256 * k:256 * k + 256], T[ka][:, 0:256].indirect(T.lku[:, 16 * k:16 * k + 16]), T[me][:], A.subtract),
               256, (ka, me, "lku"), ("df%d" % k,))
        for c in range(2):
            S(act(T.da[:, 1024 * c:1024 * c + 1024], T.df[:, 1024 * c:1024 * c + 1024], F.Abs), 1024,
              ["df%d" % k for k in range(4 * c, 4 * c + 4)], ("da%d" % c,))
        for q in range(4):
            P(mms([(T[pbank][:, 128 * q:128 * q + 128], T["bq%d" % q][:, 15 - p:143 - p], T.da[:, p::16], p == 0, p == 15)
                   for p in range(16)]), 2048, ("da0", "da1", "bq%d" % q), ("cq%d" % q,), (pbank,))
        for q in range(4):
            V(tt(T.ky[:, q, :], T[pbank][:, 128 * q:128 * q + 128], T.kw[:], A.add), 128, ("cq%d" % q, "kw"), ("ky%d" % q,), (pbank,))
        V(tt(T.k1[:], T.ky[:, :, 0:64], T.ky[:, :, 64:128], A.min), 512, ["ky%d" % q for q in range(4)], ("k1",))
        V(tt(T.k2[:], T.k1[:, :, 0:32], T.k1[:, :, 32:64], A.min), 256, ("k1",), ("k2",))
        V(tt(T.k3[:], T.k2[:, :, 0:16], T.k2[:, :, 16:32], A.min), 128, ("k2",), ("k3",))
        V(cp(T.q1[:], T.k3[:]), 64, ("k3",), ("q1",))
        V(ts(T.q2[:], T.q1[:], 255, A.bitwise_and), 64, ("q1",), ("q2",))

    choose("a0b", "pb0")
    V(cp(T.oh[:], T.q2[:]), 64, ("q2",), ("oh",))
    V(cp(T.f0[:], T.ci[:]), 256, ("ci",), ("f0",))

    V(ts(T.kt[:, 0, :], T.kc[:], 255, A.bitwise_and), 256, ("kc",), ("kt0",))
    V(ts(T.kt[:, 1, :], T.kc[:], 8, A.arith_shift_right), 256, ("kc",), ("kt1",))
    V(ts(T.kt[:, 2, :], T.uc[:], 255, A.bitwise_and), 256, ("uc",), ("kt2",))
    V(ts(T.kt[:, 3, :], T.uc[:], 8, A.arith_shift_right), 256, ("uc",), ("kt3",))
    BST[0] = 40.0
    V(ts(T.kf[:, 4, :], T.kc[:], 0.0, A.is_ge), 256, ("kc",), ("kf4",))
    BST[0] = 0.0
    for f in (4, 0, 1, 2, 3):
        if f < 4:
            V(cp(T.kf[:, f, :], T.kt[:, f, :]), 256, ("kt%d" % f,), ("kf%d" % f,))
        D(T.mkr[:] if f == 4 else T.ku[f:128:16, :], T.kf[:, f, :], ("kf%d" % f,), ("ku%d" % f,))
    for k in range(8):
        pn = ("pb1", "pc1", "pb0", "pc0")[k % 4]
        P(mms([(T[pn][:], T.rm[:], T.mkr[:, 512 * k:512 * k + 512], True, True)]), 512, ("rm", "ku4"), ("mk%d" % (k % 4),), (pn,))
        V(tt(T.st[:, 512 * k:512 * k + 512], T[pn][:], T.sraw[:, 512 * k:512 * k + 512], A.mult), 512,
          ("mk%d" % (k % 4), "sraw"), ("st%d" % k,), (pn,))
    st_r = ["st%d" % k for k in range(8)]
    V(cp(T.uf[:], T.bu[:, 0::2]), 128, ["bu%d" % i for i in range(8)], ("uf",))
    P(mms([(T.pb1[:, 0:128], T.uf[:], T.idf[:], True, True)]), 512, ("uf", "idf"), ("upp",), ("pb1",))
    V(cp(T.upl[:], T.pb1[:, 0:128]), 128, ("upp",), ("upl",), ("pb1",))
    for c in range(4):
        SG(lambda c=c: g.scalar.activation(T.sp[:, 512 * c:512 * c + 512], T.sraw[:, 0:4096].indirect(T.upl[:, 32 * c:32 * c + 32]), F.Copy),
           512, ("sraw", "upl"), ("sp%d" % c,))
    V(ms(T.sp[:, 0:1], 255.0), 1, (), ("sp0",))

    def spread(h):
        b, p = "al%d" % ((rank - h) % NR), str(h % 2)
        for k in range(8):
            if h == 0:
                S(act(T["ax" + p][:, k::8], T[b][:]), 256, (b,), ("ax%s.%d" % (p, k),))
            else:
                G(sel(T["ax" + p][:, k::8], T[b][:], [[0, 256]], A.is_ge, 0.0, 1, 0), 256, (b,), ("ax%s.%d" % (p, k),))
        for vb in range(2):
            for vh in range(4):
                for q in range(2):
                    sl = 8 * vb + 4 * q + vh
                    G(sel(T["ac" + p][:, sl::16], T[b][:, 64 * vh + vb:64 * vh + 64:2], [[0, 32]], A.is_ge, 0.0, 1, 0),
                      32, (b,), ("ac%s.%d" % (p, sl),))

    def half(h, H):
        s = str(H)
        p = str(h % 2)
        K = lambda n: n + s
        pa, pb, pc, pe = T["pa" + s], T["pb" + s], T["pc" + s], T["pe" + s]
        PA, PB, PC, PE = "pa" + s, "pb" + s, "pc" + s, "pe" + s
        tx = pa[:, 0:8, :]
        win, wk = (T.f0, "f0") if h == 0 else (T["fw" + s], K("fw"))
        ok = "oh" if h == 0 else "ow%d" % ((rank - h) % NR)
        off = T[ok]
        gg, x, wt, qq = T["gg" + s], T["x" + s], T["w" + s], T["qq" + s]
        SG(lambda: g.scalar.activation(gg[:], win[:, 0:256].indirect(off[:, 32 * H:32 * H + 32]), F.Copy), 512, (wk, ok), (K("gg"),))
        lst, rr = [], []
        for q in range(2):
            for vb in range(2):
                n = "sel%d" % (2 * H + q if h == 0 else q)
                rr.append(n)
                c = 8 * vb + 4 * q
                lst.append((pa[:, 0:8, c:c + 4], gg[:, 256 * q + vb:256 * q + 256:2], T[n][:], True, True))
        P(mms(lst), 1024, [K("gg")] + rr, (K("tx"),), (PA,))
        S(act(x[:, 0:128], tx), 128, (K("tx"),), (K("x"),), (PA,))
        P(mms([(pb[:, 0:128], x[:, 0:128], T.idf[:], True, True)]), 512, (K("x"), "idf"), (K("ll"),), (PB,))
        sl = T["sl" + s]
        V(cp(sl[:], pb[:, 0:128]), 128, (K("ll"),), (K("sl"),), (PB,))
        pd = T["pd" + s]
        VG(tt(pd[:], T.st[:, 0:4096].indirect(sl[:]), T["ax" + p][:], A.mult), 2048,
           st_r + [K("sl")] + ["ax%s.%d" % (p, k) for k in range(8)], (K("pd"),))
        ub = T["yy" + s][:, 0:128]
        S(act(ub, tx, F.Copy, BIG, 1.0 - 2.0 ** -13), 128, (K("tx"),), (K("ub"),), (PA,))
        S(act(pc[:, 0:128], ub, F.Copy, -BIG), 128, (K("ub"),), (K("U"),), (PC,))
        S(act(x[:, 128:256], tx), 128, (K("tx"),), (K("xx"),), (PA,))
        P(mms([(pe[:, 0:16, :], T.nid[:], x[:], True, False)]), 1024, (K("x"), K("xx"), "nid"), (K("kr"),), (PE,))
        P(mms([(pb[:, 128 + i:256:16], pd[:, i::16], T.ind[:, 0::4], True, True) for i in range(16)]), 4096,
          (K("pd"), "ind"), (K("er"),), (PB,))
        key, mx = W(H, "key"), fld(H, "mx", 3)
        V(tt(key, pb[:, 128:256], T.tb[:], A.add), 128, (K("er"), "tb"), (K("key"),), (PB,))
        V(lambda: g.vector.tensor_tensor_scan(W(H, "mx"), T.rs[:], key, 0.0, A.mult, A.max), 128, (K("key"), "rs"), (K("mx"),))
        for t in range(4):
            S(act(fld(H, "mr", t), mx), 32, (K("mx"),), (K("mr%d." % t),))
        for t in range(4):
            V(tt(fld(H, "Z", t), fld(H, "key", t), mx, A.is_equal), 64, (K("key"), K("mx")), (K("Z%d." % t),))
        Zr = [K("Z%d." % t) for t in range(4)]
        V(tt(W(H, "um"), pc[:, 0:128], W(H, "Z"), A.add), 128, Zr + [K("U")], (K("um"),), (PC,))
        U = [fld(H, "um", t) for t in range(4)]
        Q = [qq[:, t:128:4] for t in range(4)]
        J = [fld(H, "J", t) for t in range(4)]
        e02, e03, e13, e12 = fld(H, "d5", 0), fld(H, "d2", 0), fld(H, "d2", 1), fld(H, "d2", 2)
        um = (K("um"),)
        V(tt(e02, U[0], U[2], A.is_equal), 64, um, (K("e02"),))
        V(tt(e03, U[0], U[3], A.is_equal), 64, um, (K("e03"),))
        V(tt(Q[1], U[0], U[1], A.is_equal), 64, um, (K("Q1"),))
        V(tt(e13, U[1], U[3], A.is_equal), 64, um, (K("e13"),))
        V(tt(e12, U[1], U[2], A.is_equal), 64, um, (K("e12"),))
        V(tt(J[2], U[2], U[3], A.is_equal), 64, um, (K("J2"),))
        V(tt(J[0], e02, e03, A.add), 64, (K("e02"), K("e03")), (K("J0"),))
        V(tt(J[1], e13, e12, A.add), 64, (K("e13"), K("e12")), (K("J1"),))
        V(tt(J[0], J[0], Q[1], A.add), 64, (K("J0"), K("Q1")), (K("J0"),))
        Jr = [K("J%d" % t) for t in range(4)]
        Qr = [K("Q%d" % t) for t in range(4)]
        V(tt(W(H, "ju"), pc[:, 0:128], W(H, "J"), A.mult), 128, Jr + [K("U")], (K("ju"),), (PC,))
        o = 128 * WN.index("ju")
        lk, ct = T["lk_" + s], T["ct" + s]
        V(tt(wt[:, o:o + 128:4], wt[:, o:o + 128:4], wt[:, o + 1:o + 128:4], A.add), 64, (K("ju"),), (K("jua"),))
        V(tt(ct[:, 3:131:4], wt[:, o:o + 128:4], wt[:, o + 2:o + 128:4], A.add), 64, (K("ju"), K("jua")), (K("CT"),))
        P(mms([(pb[:, 320:352], ct[:, 3 - v:131 - v], T.idf[:, 32 * v:32 * v + 32], v == 0, v == 3) for v in range(4)]), 1024,
          (K("CT"), "idf"), (K("cl"),), (PB,))
        V(tt(W(H, "zc"), tx, W(H, "Z"), A.mult), 128, Zr + [K("tx")], (K("zc"),), (PA,))
        oz = 128 * WN.index("zc")
        V(tt(wt[:, oz:oz + 128:2], wt[:, oz:oz + 128:2], wt[:, oz + 1:oz + 128:2], A.add), 128, (K("zc"),), (K("zc"),))
        V(tt(lk[:, 2:130:4], wt[:, oz:oz + 128:4], wt[:, oz + 2:oz + 128:4], A.add), 64, (K("zc"),), (K("LK0"),))
        P(mms([(pb[:, 256:320], y[:, 2 - 2 * v:130 - 2 * v], T.idf[:, 64 * v:64 * v + 64], v == 0 and y is lk, v == 1 and y is ct)
               for y in (lk, ct) for v in range(2)]), 1024, (K("LK0"), K("CT"), "idf"), (K("kl"),), (PB,))
        li = T["lst" + s]
        V(ts(li[:, 64:96], pb[:, 320:352], 0.5, A.mult), 64, (K("cl"),), (K("lc"),), (PB,))
        V(cp(li[:, 0:64], pb[:, 256:320]), 64, (K("kl"),), (K("lu"),), (PB,))
        ko, pr = T["ko" + s], T["pr" + s]
        SG(lambda: g.scalar.activation(ko[:], T.ku[:, 0:4096].indirect(li[:, 0:64]), F.Copy), 1024,
           [K("lu")] + ["ku%d" % f for f in range(4)], (K("ko"),))
        VG(tt(pr[:], T.sp[:, 0:2048].indirect(li[:, 64:96]), T["ac" + p][:], A.mult), 512,
           [K("lc")] + ["sp%d" % c for c in range(4)] + ["ac%s.%d" % (p, i) for i in range(16)], (K("pr"),))
        P(mms([(pa[32 * v:32 * v + 32, 8:16, 4 * i:4 * i + 4], pr[:, 4 * i + v::16], T.ind[:], True, True)
               for v in range(4) for i in range(4)]), 2048, (K("pr"), "ind"), (K("co"),), (PA,))
        V(tt(Q[2], e02, e12, A.add), 64, (K("e02"), K("e12")), (K("Q2"),))
        V(tt(Q[3], e13, e03, A.add), 64, (K("e13"), K("e03")), (K("Q3"),))
        V(tt(Q[3], Q[3], J[2], A.add), 64, (K("Q3"), K("J2")), (K("Q3"),))
        V(tt(W(H, "S"), qq[:, 0:128], W(H, "Z"), A.add), 256, Zr + Qr, (K("S"),))
        P(mms([(pe[64 * v:64 * v + 64, 8 * kind:8 * kind + 8, 4 * i:4 * i + 4], ko[:, 4 * i + 2 * v + kind::16],
                (T.wk, T.wu)[kind][:], False, False) for v in range(2) for i in range(4) for kind in range(2)]
              + [(pe[:, 0:16, :], T.idb[:], qq[:], False, True)]), 1280, [K("ko"), "wk", "wu", "idb"] + Qr, (K("kr"),), (PE,))
        V(tt(W(H, "go"), pa[:, 8:16, :], W(H, "mr"), A.is_lt), 128, [K("co")] + [K("mr%d." % t) for t in range(4)], (K("go"),), (PA,))
        V(tt(pc[:, 256:384], pe[:, 0:8, :], W(H, "S"), A.mult), 128, (K("kr"), K("S")), (K("d1"),), (PE, PC))
        V(tt(W(H, "d2"), pe[:, 8:16, :], W(H, "J"), A.mult), 128, [K("kr")] + Jr, (K("d2"), K("e03"), K("e13"), K("e12")), (PE,))
        V(tt(pc[:, 384:512], pc[:, 256:384], W(H, "d2"), A.add), 128, (K("d1"), K("d2")), (K("d4"),), (PC,))
        V(tt(W(H, "d5"), pc[:, 384:512], W(H, "go"), A.mult), 128, (K("d4"), K("go")), (K("d5"), K("e02")), (PC,))
        t3 = T["t3" + s]
        V(tt(t3[:, 0:128], tx, W(H, "d5"), A.add), 128, (K("d5"), K("e02"), K("tx")), (K("T3"),), (PA,))
        P(mms([(pe[:, 16:24, :], t3[:, 0:128], T.idf[:], True, True), (pe[:, 24:32, :], t3[:, 8:136], T.idf[:], True, True)]), 1024,
          (K("T3"), K("T3p"), "idf"), (K("nf"),), (PE,))
        fw, ml, mg = T["fw" + s], T["ml" + s], T["mg" + s][:, 2048 * (h % 2):2048 * (h % 2) + 2048]
        S(act(fw[:], pe[:, 16:32, :]), 256, (K("nf"),), (K("fw"),), (PE,))
        V(cp(ml[:], fw[:, 0:128]), 128, (K("fw"),), (K("ml"),))
        if h == NR - 1:
            yy = T["yy" + s]
            S(act(yy[:, 0::2], fw[:, 0:128]), 128, (K("fw"),), (K("ya"), K("ub")))
            S(act(yy[:, 1::2], fw[:, 128:256]), 128, (K("fw"),), (K("yb"), K("ub")))
            for i in range(8):
                D(T.yc[8 * H + i:128:16, :], yy[i:128:16, :], (K("ya"), K("yb")), ())
        BST[0] = PBG
        cw = 2048 // CM
        for c in range(CM):
            o_, l_ = mg[:, cw * c:cw * c + cw], ml[:, cw // 16 * c:cw // 16 * (c + 1)]
            if h == NR - 1 and c >= CM // 2:
                VG(cp(o_, T.mt[:, 0:4096].indirect(l_)), cw, ("mt", K("ml")), (K("mg%d.%s." % (c, p)),))
            else:
                SG(lambda o_=o_, l_=l_: g.scalar.activation(o_, T.mt[:, 0:4096].indirect(l_), F.Copy), cw,
                   ("mt", K("ml")), (K("mg%d.%s." % (c, p)),))
        BST[0] = 0.0

    def msum(h):
        n = 0
        for H in range(2):
            mg = T["mg%d" % H][:, 2048 * (h % 2):2048 * (h % 2) + 2048]
            for part in range(2):
                lst = []
                for k in range(4 * part, 4 * part + 4):
                    lst.append((T.pa1[:, 16:32, :], T.idb[:], mg[:, k::8], n == 0, n == 15))
                    n += 1
                P(mms(lst), 1024, ["mg%d.%d.%d" % (c, h % 2, H) for c in range(CM)] + ["idb"], ("msp",), ("pa1",))
        S(act(T["ms%d" % h][:], T.pa1[:, 16:32, :]), 256, ("msp",), ("ms%d" % h,), ("pa1",))
        if h:
            b = (rank - h) % NR
            add("G", send(T.cores[b], "ms%d" % h, "el%d" % h, "ee%d" % h), 0.3, ("ms%d" % h,), ("se%d" % h,), (), 4.0, "remote")

    spread(0)
    half(0, 0)
    half(0, 1)
    choose("al%d" % nxt, "pb0")
    V(ts(T.q3[:], T.q2[:], 1, A.arith_shift_right), 64, ("q2",), ("q3",))
    V(ts(T.q4[:], T.q2[:], 1, A.bitwise_and), 64, ("q2",), ("q4",))
    V(ts(T.ys[:, 0:64], T.q4[:], 128.0, A.mult), 64, ("q4",), ("q5",))
    V(tt(T.ys[:, 64:128], T.q3[:], T.ys[:, 0:64], A.add), 128, ("q3", "q5"), ("q6",))
    V(cp(T["ow%d" % rank][:], T.ys[:, 64:128]), 64, ("q6",), ("ow%d" % rank,))
    add("G", bcast("ow%d" % rank, "oo%d" % rank), 0.5, ("ow%d" % rank,), ("so",), (), 3.0, "remote")
    for h in range(1, NR):
        b = (rank - h) % NR
        arrive("ow%d" % b, "oo%d" % b, "so")
    for h in range(1, NR):
        spread(h)
        half(h, 0)
        half(h, 1)
        msum(h - 1)
    msum(NR - 1)
    for h in range(1, NR):
        arrive("el%d" % h, "ee%d" % h, "se%d" % h)
    src = ["ms0"] + ["el%d" % h for h in range(1, NR)]
    for i, n in enumerate(src):
        P(mms([(T.pb0[:, 0:256], T.idf[:], T[n][:], i == 0, i == 7)]), 1024, (n, "idf"), ("ef",), ("pb0",))
    V(tt(T.ys[:], T.pb0[:, 0:256], T[me][:], A.mult), 256, ("ef", me), ("ys", "q5", "q6"), ("pb0",))
    D(T.ye[:], T.ys[:], ("ys",), (), eng="A")

    emit(g, T, ops, ne, nloc)


def emit(g, T, ops, ne, nloc):
    n = len(ops)
    succ = [[] for _ in range(n)]
    indeg = [0] * n
    for i, o in enumerate(ops):
        for j in o["deps"]:
            succ[j].append(i)
            indeg[i] += 1
    prio = [0.0] * n
    for i in range(n - 1, -1, -1):
        prio[i] = ops[i]["dur"] + ops[i]["lat"] + max([prio[j] + HOP for j in succ[i]], default=0.0)
    ready = [0.0] * n
    free = {"V": 0.0, "A": 0.0, "P": 0.0, "G": 0.0, "S": 0.0, "X": 0.0}
    avail = {e: [] for e in free}
    for i in range(n):
        if indeg[i] == 0:
            avail[ops[i]["eng"]].append(i)
    order = []
    while len(order) < n:
        best = None
        for e, lst in avail.items():
            if not lst:
                continue
            if e == "X":
                c = min(lst, key=lambda i: ready[i])
                st = ready[c]
            else:
                s0 = min(max(free[e], ready[i]) for i in lst)
                c = max((i for i in lst if max(free[e], ready[i]) <= s0 + TOL),
                        key=lambda i: (ops[i]["sem"] == "remote", prio[i] + ops[i]["pb"], -i))
                st = max(free[e], ready[c])
            if best is None or st < best[0]:
                best = (st, e, c)
        st, e, c = best
        avail[e].remove(c)
        fin = st + ops[c]["dur"]
        if e != "X":
            free[e] = fin
        order.append(c)
        for j in succ[c]:
            same = ops[j]["eng"] == e and not ops[j]["deps"][c]
            ready[j] = max(ready[j], st if same else fin + ops[c]["lat"] + HOP)
            indeg[j] -= 1
            if indeg[j] == 0:
                avail[ops[j]["eng"]].append(j)
    queue = {"V": g.vector, "A": g.scalar, "P": g.tensor, "G": g, "S": g.sync}
    count = {"V": 0, "A": 0, "P": 0, "G": 0}
    done = [None] * n
    know = {e: {} for e in queue}
    snap = [None] * n
    for c in order:
        o = ops[c]
        e = o["eng"]
        if e == "X":
            done[c] = (o["sem"], ne)
            snap[c] = {}
            continue
        kn = know[e]
        need = {}
        for j, wait in sorted(o["deps"].items()):
            if wait:
                sname, v = done[j]
                if kn.get(sname, 0) < v and need.get(sname, (0, 0))[0] < v:
                    need[sname] = (v, j)
        for sname, (v, j) in sorted(need.items(), key=lambda kv: -kv[1][1]):
            if kn.get(sname, 0) >= v:
                continue
            queue[e].wait_ge(T.sem[sname], v)
            kn[sname] = v
            for k2, v2 in snap[j].items():
                if kn.get(k2, 0) < v2:
                    kn[k2] = v2
        snap[c] = dict(kn)
        ins = o["fn"]()
        if o["sem"] == "remote":
            done[c] = None
            continue
        if o["sem"] is not None:
            ins.then_inc(T.sem[o["sem"]], 16)
            done[c] = (o["sem"], 16)
        else:
            count[e] += 1
            ins.then_inc(T.sem[CTR[e]], 1)
            done[c] = (CTR[e], count[e])
    g.wait_ge(T.sem.loc, nloc[0])
    for i in range(n):
        d = done[i]
        if d is not None and know["G"].get(d[0], 0) < d[1]:
            tot = count[[k for k in CTR if CTR[k] == d[0]][0]] if d[0] in CTR.values() else d[1]
            g.wait_ge(T.sem[d[0]], tot)
            know["G"][d[0]] = tot
